import numpy as np
import ml_dtypes


def mxq(x, axis, fmt="e4m3"):
    dtype, down = {"e4m3": (ml_dtypes.float8_e4m3fn, 7), "e5m2": (ml_dtypes.float8_e5m2, 14)}[fmt]
    v = np.moveaxis(np.asarray(x, np.float32).astype(ml_dtypes.bfloat16).astype(np.float64), axis, -1)
    blocks = v.reshape(v.shape[:-1] + (-1, 32))
    amax = np.abs(blocks).max(-1, keepdims=True)
    byte = np.maximum(np.where(amax > 0, np.frexp(amax)[1] - 1 + 127, 0) - down, 1)
    scale = np.exp2(byte - 127.0)
    codes = (blocks / scale).astype(np.float32).astype(dtype).astype(np.float64)
    return np.moveaxis((codes * scale).reshape(v.shape), -1, axis)


WIDE = False


def mx_kscale(k, group=512):
    if not WIDE:
        return np.ones(k)
    levels = np.array([18, -18])
    if group != 512:
        return np.exp2(np.random.permutation(np.resize(levels, k // group))).repeat(group)
    if k % 512:
        return np.exp2(np.random.permutation(np.resize(levels, k // 32))).repeat(32)
    a = np.empty((k // 512, 16))
    for p in range(k // 512):
        a[p, :8] = np.random.permutation(np.resize(levels, 8))
        for g in range(8):
            far = levels[np.abs(levels - a[p, g]) >= 10]
            a[p, g + 8] = far[np.random.randint(len(far))]
    return np.exp2(a.ravel()).repeat(32)


def f64(x):
    return np.asarray(x).astype(np.float64)


G, D, M, O, N = 4, 128, 128, 128, 512


def setup_inputs():
    n = np.random.standard_normal
    s_d = mx_kscale(D, 0)
    s_o = mx_kscale(O, 0)
    return {
        "x": (n((G, D, N)) * s_d[:, None]).astype(np.float32),
        "w1": (n((G, D, M)) / np.sqrt(D) / s_d[:, None]).astype(np.float32),
        "w2": (n((G, D, M)) / np.sqrt(D) / s_d[:, None]).astype(np.float32),
        "w3": (n((G, D, M)) / np.sqrt(D) / s_d[:, None]).astype(np.float32),
        "wo": (n((G, O, M)) / np.sqrt(O) / s_o[:, None]).astype(np.float32),
        "dy": (n((G, O, N)) * s_o[:, None]).astype(np.float32),
        "old": (0.3 * n((G, M, N))).astype(np.float32),
    }


def reference(x, w1, w2, w3, wo, dy, old):
    w1q = mxq(f64(w1), 1, "e4m3")
    xq = mxq(f64(x), 1, "e4m3")
    z1 = w1q.transpose(0, 2, 1) @ xq
    w2q = mxq(f64(w2), 1, "e4m3")
    z2 = w2q.transpose(0, 2, 1) @ xq
    w3q = mxq(f64(w3), 1, "e4m3")
    z3 = w3q.transpose(0, 2, 1) @ xq
    se = np.exp(z1) + np.exp(z2) + np.exp(z3)
    woq = mxq(f64(wo), 1, "e4m3")
    dyq = mxq(f64(dy), 1, "e4m3")
    c0 = woq.transpose(0, 2, 1) @ dyq
    dse = c0 * np.tanh(z1) / se
    dz1 = c0 * np.log(se) * (1.0 - np.square(np.tanh(z1))) + dse * np.exp(z1)
    y = dz1 + f64(old)
    return y

@@ -1,0 +1,242 @@
+from contextlib import ExitStack
+
+import concourse.mybir as mybir
+
+G, D, M, N = 4, 128, 128, 512
+FLOPS = 4 * 2 * G * D * M * N
+
+F32 = mybir.dt.float32
+BF16 = mybir.dt.bfloat16
+U32 = mybir.dt.uint32
+U8 = mybir.dt.uint8
+FP8X4 = mybir.dt.float8_e4m3fn_x4
+ACT = mybir.ActivationFunctionType
+ALU = mybir.AluOpType
+
+P = 128
+PACK = 4
+ROWS = 32
+X_SPLIT = 352
+
+
+def tile_rows_bsoftmaxthree_kernel(tc, x, w1, w2, w3, wo, dy, old, out):
+    nc = tc.nc
+    with ExitStack() as ctx:
+        sb = ctx.enter_context(tc.tile_pool(name="sb", bufs=1))
+        ps = ctx.enter_context(tc.psum_pool(name="ps", bufs=1))
+        ctx.enter_context(tc.manual_schedule())
+
+        def load(name, src, width):
+            raw = sb.tile([P, PACK, width], F32, name=name, align_bytes=64)
+            rows = src.rearrange("g d c -> (g d) c").rearrange("(p j) c -> p j c", j=PACK)
+            nc.sync.dma_start(out=raw[:], in_=rows)
+            return raw
+
+        def operand(name, width):
+            rounded = sb.tile([P, width, PACK], BF16, name=name + "_bf", align_bytes=64)
+            codes = sb.tile([P, width], U32, name=name + "_codes", align_bytes=64)
+            scales = sb.tile([P, width], U8, name=name + "_scales", align_bytes=64)
+            return rounded, codes, scales
+
+        def views(op, at, raw, lo, hi):
+            dst = op[0][:, at + lo : at + hi, :].rearrange("p (c i) j -> p c j i", i=4)
+            src = raw[:, :, lo:hi].rearrange("p j (c i) -> p c j i", i=4)
+            return dst, src
+
+        def quantize(op):
+            nc.vector.quantize_mx(out=op[1][:].bitcast(FP8X4), scales=op[2][:], in_=op[0][:].rearrange("p c j -> p (c j)"))
+
+        def product(bank, g, weights, at, moving, start, stop):
+            rows = slice(ROWS * g, ROWS * (g + 1))
+            nc.tensor.matmul_mx(
+                out=bank[:],
+                lhsT=weights[1][rows, at : at + M].bitcast(FP8X4),
+                lhsT_scale=weights[2][rows, at : at + M],
+                rhs=moving[1][rows, :].bitcast(FP8X4),
+                rhs_scale=moving[2][rows, :],
+                start=start,
+                stop=stop,
+            )
+
+        def per_group(name):
+            return [sb.tile([P, N], F32, name=name + str(g), align_bytes=64) for g in range(G)]
+
+        w1_raw = load("w1_raw", w1, M)
+        x_raw = load("x_raw", x, N)
+        w2_raw = load("w2_raw", w2, M)
+        w3_raw = load("w3_raw", w3, M)
+        wo_raw = load("wo_raw", wo, M)
+        dy_raw = load("dy_raw", dy, N)
+        old_sb = sb.tile([P, G, N], F32, name="old_sb", align_bytes=64)
+        nc.sync.dma_start(out=old_sb[:], in_=old.rearrange("g m n -> m g n"))
+
+        w1_op = operand("w1", 2 * M)
+        w23_op = operand("w23", 2 * M)
+        wo_op = operand("wo", M)
+        x_op = operand("x", N)
+        dy_op = operand("dy", N)
+
+        bank_a = [ps.tile([P, N], F32, name="bank_a" + str(g)) for g in range(G)]
+        bank_b = [ps.tile([P, N], F32, name="bank_b" + str(g)) for g in range(G)]
+        th = per_group("th")
+        sq = per_group("sq")
+        e2 = per_group("e2")
+        e3 = per_group("e3")
+        esum = per_group("esum")
+        ct = per_group("ct")
+        negA = per_group("negA")
+        lnq = per_group("lnq")
+        lse = per_group("lse")
+        p1 = per_group("p1")
+        mm = per_group("mm")
+        part = per_group("part")
+        nn = per_group("nn")
+        res = per_group("res")
+
+        dst, src = views(w1_op, 0, w1_raw, 0, M)
+        nc.vector.tensor_copy(out=dst, in_=src)
+        dst, src = views(w1_op, M, w1_raw, 0, M)
+        nc.vector.tensor_scalar(out=dst, in0=src, scalar1=-1.0, scalar2=None, op0=ALU.mult)
+        quantize(w1_op)
+        dst, src = views(x_op, 0, x_raw, X_SPLIT, N)
+        nc.scalar.activation(out=dst, in_=src, func=ACT.Copy)
+        dst, src = views(x_op, 0, x_raw, 0, X_SPLIT)
+        nc.vector.tensor_copy(out=dst, in_=src)
+        quantize(x_op)
+        for g in range(G):
+            product(bank_a[g], g, w1_op, 0, x_op, True, True)
+        dst, src = views(w23_op, 0, w2_raw, 0, M)
+        nc.scalar.activation(out=dst, in_=src, func=ACT.Copy)
+        dst, src = views(w23_op, M, w3_raw, 0, M)
+        nc.scalar.activation(out=dst, in_=src, func=ACT.Copy)
+        quantize(w23_op)
+
+        def diff(banks, at, pair):
+            for g in pair:
+                product(banks[g], g, w23_op, at, x_op, True, False)
+            for g in pair:
+                product(banks[g], g, w1_op, M, x_op, False, True)
+
+        def f_tanh(g):
+            nc.scalar.activation(out=th[g][:], in_=bank_a[g][:], func=ACT.Tanh)
+
+        def f_sq_v(g):
+            nc.vector.tensor_tensor(out=sq[g][:], in0=th[g][:], in1=th[g][:], op=ALU.mult)
+
+        def f_sq_s(g):
+            nc.scalar.activation(out=sq[g][:], in_=th[g][:], func=ACT.Square)
+
+        def f_e2(g):
+            nc.scalar.activation(out=e2[g][:], in_=bank_b[g][:], func=ACT.Exp)
+
+        def f_e3(g):
+            nc.scalar.activation(out=e3[g][:], in_=bank_a[g][:], func=ACT.Exp)
+
+        def f_D(g, eng):
+            eng.tensor_tensor(out=esum[g][:], in0=e2[g][:], in1=e3[g][:], op=ALU.add)
+
+        def f_c0(g):
+            product(bank_b[g], g, wo_op, 0, dy_op, True, True)
+
+        def f_z1(g):
+            product(bank_a[g], g, w1_op, 0, x_op, True, True)
+
+        def f_ct(g):
+            nc.vector.tensor_tensor(out=ct[g][:], in0=bank_b[g][:], in1=th[g][:], op=ALU.mult)
+
+        def f_A(g):
+            nc.vector.scalar_tensor_tensor(out=negA[g][:], in0=sq[g][:], scalar=1.0, in1=bank_b[g][:], op0=ALU.subtract, op1=ALU.mult)
+
+        def f_ln(g):
+            nc.scalar.activation(out=lnq[g][:], in_=esum[g][:], func=ACT.Ln, bias=1.0)
+
+        def f_L(g):
+            nc.vector.tensor_tensor(out=lse[g][:], in0=bank_a[g][:], in1=lnq[g][:], op=ALU.add)
+
+        def f_r(g):
+            nc.scalar.activation(out=p1[g][:], in_=lnq[g][:], func=ACT.Exp, scale=-1.0)
+
+        def f_m(g, eng):
+            eng.tensor_tensor(out=mm[g][:], in0=negA[g][:], in1=lse[g][:], op=ALU.mult)
+
+        def f_part(g):
+            nc.vector.tensor_tensor(out=part[g][:], in0=old_sb[:, g, :], in1=mm[g][:], op=ALU.subtract)
+
+        def f_n(g, lo, hi):
+            nc.vector.tensor_tensor(out=nn[g][:, lo:hi], in0=ct[g][:, lo:hi], in1=p1[g][:, lo:hi], op=ALU.mult)
+
+        def f_out(g, lo, hi):
+            nc.vector.tensor_tensor(out=res[g][:, lo:hi], in0=nn[g][:, lo:hi], in1=part[g][:, lo:hi], op=ALU.add)
+            nc.sync.dma_start(out=out[g, :, lo:hi], in_=res[g][:, lo:hi])
+
+        diff(bank_b, 0, (0, 1))
+        for g in range(G):
+            f_tanh(g)
+        diff(bank_a, M, (0, 1))
+        diff(bank_b, 0, (2, 3))
+        diff(bank_a, M, (2, 3))
+
+        dst, src = views(wo_op, 0, wo_raw, 0, M)
+        nc.vector.tensor_copy(out=dst, in_=src)
+        f_sq_v(0)
+        quantize(wo_op)
+        dst, src = views(dy_op, 0, dy_raw, 0, N)
+        nc.vector.tensor_copy(out=dst, in_=src)
+        f_sq_v(1)
+        quantize(dy_op)
+
+        f_e2(0)
+        f_e2(1)
+        f_c0(0)
+        f_c0(1)
+        f_e3(0)
+        f_e3(1)
+        f_z1(0)
+        f_z1(1)
+        f_e2(2)
+        f_e2(3)
+        f_c0(2)
+        f_c0(3)
+        f_e3(2)
+        f_e3(3)
+        f_z1(2)
+        f_z1(3)
+        f_sq_s(2)
+        f_sq_s(3)
+        f_D(0, nc.vector)
+        f_D(1, nc.vector)
+        f_ct(0)
+        f_ct(1)
+        f_A(0)
+        f_A(1)
+        f_ct(2)
+        f_D(2, nc.vector)
+        f_ct(3)
+        f_D(3, nc.vector)
+        f_A(2)
+        f_A(3)
+        for g in range(G):
+            f_ln(g)
+        for g in range(G):
+            f_r(g)
+        f_L(0)
+        f_L(1)
+        f_m(0, nc.vector)
+        f_L(2)
+        f_m(1, nc.vector)
+        f_L(3)
+        f_part(0)
+        f_m(2, nc.vector)
+        f_part(1)
+        f_m(3, nc.vector)
+        f_n(0, 0, N)
+        f_part(2)
+        f_out(0, 0, N)
+        f_n(1, 0, N)
+        f_part(3)
+        f_out(1, 0, N)
+        f_n(2, 0, N)
+        f_n(3, 0, N)
+        f_out(2, 0, N)
+        f_out(3, 0, N // 2)
+        f_out(3, N // 2, N)

@@ -16,7 +16,8 @@ ALU = mybir.AluOpType
 P = 128
 PACK = 4
 ROWS = 32
-X_SPLIT = 352
+HALF = N // 2
+X_SPLIT = 176
 
 
 def tile_rows_bsoftmaxthree_kernel(tc, x, w1, w2, w3, wo, dy, old, out):
@@ -26,10 +27,10 @@ def tile_rows_bsoftmaxthree_kernel(tc, x, w1, w2, w3, wo, dy, old, out):
         ps = ctx.enter_context(tc.psum_pool(name="ps", bufs=1))
         ctx.enter_context(tc.manual_schedule())
 
-        def load(name, src, width):
-            raw = sb.tile([P, PACK, width], F32, name=name, align_bytes=64)
+        def load(name, src, lo, hi):
+            raw = sb.tile([P, PACK, hi - lo], F32, name=name, align_bytes=64)
             rows = src.rearrange("g d c -> (g d) c").rearrange("(p j) c -> p j c", j=PACK)
-            nc.sync.dma_start(out=raw[:], in_=rows)
+            nc.sync.dma_start(out=raw[:], in_=rows[:, :, lo:hi])
             return raw
 
         def operand(name, width):
@@ -43,8 +44,20 @@ def tile_rows_bsoftmaxthree_kernel(tc, x, w1, w2, w3, wo, dy, old, out):
             src = raw[:, :, lo:hi].rearrange("p j (c i) -> p c j i", i=4)
             return dst, src
 
-        def quantize(op):
-            nc.vector.quantize_mx(out=op[1][:].bitcast(FP8X4), scales=op[2][:], in_=op[0][:].rearrange("p c j -> p (c j)"))
+        def round_v(op, at, raw, lo, hi):
+            dst, src = views(op, at, raw, lo, hi)
+            nc.vector.tensor_copy(out=dst, in_=src)
+
+        def round_s(op, at, raw, lo, hi):
+            dst, src = views(op, at, raw, lo, hi)
+            nc.scalar.activation(out=dst, in_=src, func=ACT.Copy)
+
+        def quantize(op, lo, hi):
+            nc.vector.quantize_mx(
+                out=op[1][:, lo:hi].bitcast(FP8X4),
+                scales=op[2][:, lo:hi],
+                in_=op[0][:, lo:hi, :].rearrange("p c j -> p (c j)"),
+            )
 
         def product(bank, g, weights, at, moving, start, stop):
             rows = slice(ROWS * g, ROWS * (g + 1))
@@ -58,17 +71,21 @@ def tile_rows_bsoftmaxthree_kernel(tc, x, w1, w2, w3, wo, dy, old, out):
                 stop=stop,
             )
 
-        def per_group(name):
-            return [sb.tile([P, N], F32, name=name + str(g), align_bytes=64) for g in range(G)]
+        def wide(name):
+            return sb.tile([P, G * N], F32, name=name, align_bytes=64)
 
-        w1_raw = load("w1_raw", w1, M)
-        x_raw = load("x_raw", x, N)
-        w2_raw = load("w2_raw", w2, M)
-        w3_raw = load("w3_raw", w3, M)
-        wo_raw = load("wo_raw", wo, M)
-        dy_raw = load("dy_raw", dy, N)
-        old_sb = sb.tile([P, G, N], F32, name="old_sb", align_bytes=64)
-        nc.sync.dma_start(out=old_sb[:], in_=old.rearrange("g m n -> m g n"))
+        def cols(g, n=1):
+            return slice(g * N, (g + n) * N)
+
+        w1_raw = load("w1_raw", w1, 0, M)
+        xa_raw = load("xa_raw", x, 0, HALF)
+        xb_raw = load("xb_raw", x, HALF, N)
+        w2_raw = load("w2_raw", w2, 0, M)
+        w3_raw = load("w3_raw", w3, 0, M)
+        wo_raw = load("wo_raw", wo, 0, M)
+        dy_raw = load("dy_raw", dy, 0, N)
+        old_sb = wide("old_sb")
+        nc.sync.dma_start(out=old_sb[:].rearrange("m (g n) -> m g n", g=G), in_=old.rearrange("g m n -> m g n"))
 
         w1_op = operand("w1", 2 * M)
         w23_op = operand("w23", 2 * M)
@@ -78,165 +95,115 @@ def tile_rows_bsoftmaxthree_kernel(tc, x, w1, w2, w3, wo, dy, old, out):
 
         bank_a = [ps.tile([P, N], F32, name="bank_a" + str(g)) for g in range(G)]
         bank_b = [ps.tile([P, N], F32, name="bank_b" + str(g)) for g in range(G)]
-        th = per_group("th")
-        sq = per_group("sq")
-        e2 = per_group("e2")
-        e3 = per_group("e3")
-        esum = per_group("esum")
-        ct = per_group("ct")
-        negA = per_group("negA")
-        lnq = per_group("lnq")
-        lse = per_group("lse")
-        p1 = per_group("p1")
-        mm = per_group("mm")
-        part = per_group("part")
-        nn = per_group("nn")
-        res = per_group("res")
+        th = wide("th")
+        sq = wide("sq")
+        e2 = wide("e2")
+        e3 = wide("e3")
+        ct = wide("ct")
+        negA = wide("negA")
+        lnq = wide("lnq")
+        lse = wide("lse")
+        p1 = wide("p1")
+        mm = wide("mm")
+        part = wide("part")
+        nn = wide("nn")
+        res = wide("res")
 
-        dst, src = views(w1_op, 0, w1_raw, 0, M)
-        nc.vector.tensor_copy(out=dst, in_=src)
+        round_v(w1_op, 0, w1_raw, 0, M)
         dst, src = views(w1_op, M, w1_raw, 0, M)
         nc.vector.tensor_scalar(out=dst, in0=src, scalar1=-1.0, scalar2=None, op0=ALU.mult)
-        quantize(w1_op)
-        dst, src = views(x_op, 0, x_raw, X_SPLIT, N)
-        nc.scalar.activation(out=dst, in_=src, func=ACT.Copy)
-        dst, src = views(x_op, 0, x_raw, 0, X_SPLIT)
-        nc.vector.tensor_copy(out=dst, in_=src)
-        quantize(x_op)
+        quantize(w1_op, 0, 2 * M)
+        round_v(x_op, 0, xa_raw, 0, HALF)
+        quantize(x_op, 0, HALF)
+        round_s(x_op, HALF, xb_raw, X_SPLIT, HALF)
+        round_v(x_op, HALF, xb_raw, 0, X_SPLIT)
+        quantize(x_op, HALF, N)
         for g in range(G):
             product(bank_a[g], g, w1_op, 0, x_op, True, True)
-        dst, src = views(w23_op, 0, w2_raw, 0, M)
-        nc.scalar.activation(out=dst, in_=src, func=ACT.Copy)
-        dst, src = views(w23_op, M, w3_raw, 0, M)
-        nc.scalar.activation(out=dst, in_=src, func=ACT.Copy)
-        quantize(w23_op)
+        round_s(w23_op, 0, w2_raw, 0, M)
+        round_s(w23_op, M, w3_raw, 0, M)
+        round_v(wo_op, 0, wo_raw, 0, M)
+        quantize(w23_op, 0, 2 * M)
+        quantize(wo_op, 0, M)
 
-        def diff(banks, at, pair):
-            for g in pair:
+        def diff(banks, at, groups):
+            for g in groups:
                 product(banks[g], g, w23_op, at, x_op, True, False)
-            for g in pair:
+            for g in groups:
                 product(banks[g], g, w1_op, M, x_op, False, True)
 
-        def f_tanh(g):
-            nc.scalar.activation(out=th[g][:], in_=bank_a[g][:], func=ACT.Tanh)
+        def f_sq(g):
+            nc.vector.tensor_tensor(out=sq[:, cols(g)], in0=th[:, cols(g)], in1=th[:, cols(g)], op=ALU.mult)
 
-        def f_sq_v(g):
-            nc.vector.tensor_tensor(out=sq[g][:], in0=th[g][:], in1=th[g][:], op=ALU.mult)
+        def f_m(eng, s):
+            eng.tensor_tensor(out=mm[:, s], in0=negA[:, s], in1=lse[:, s], op=ALU.mult)
 
-        def f_sq_s(g):
-            nc.scalar.activation(out=sq[g][:], in_=th[g][:], func=ACT.Square)
+        def f_part(s):
+            nc.vector.tensor_tensor(out=part[:, s], in0=old_sb[:, s], in1=mm[:, s], op=ALU.subtract)
 
-        def f_e2(g):
-            nc.scalar.activation(out=e2[g][:], in_=bank_b[g][:], func=ACT.Exp)
+        def f_n(s):
+            nc.vector.tensor_tensor(out=nn[:, s], in0=ct[:, s], in1=p1[:, s], op=ALU.mult)
 
-        def f_e3(g):
-            nc.scalar.activation(out=e3[g][:], in_=bank_a[g][:], func=ACT.Exp)
+        def f_out(s):
+            nc.vector.tensor_tensor(out=res[:, s], in0=nn[:, s], in1=part[:, s], op=ALU.add)
 
-        def f_D(g, eng):
-            eng.tensor_tensor(out=esum[g][:], in0=e2[g][:], in1=e3[g][:], op=ALU.add)
+        def store(g, lo, hi):
+            nc.sync.dma_start(out=out[g, :, lo:hi], in_=res[:, g * N + lo : g * N + hi])
 
-        def f_c0(g):
-            product(bank_b[g], g, wo_op, 0, dy_op, True, True)
-
-        def f_z1(g):
-            product(bank_a[g], g, w1_op, 0, x_op, True, True)
-
-        def f_ct(g):
-            nc.vector.tensor_tensor(out=ct[g][:], in0=bank_b[g][:], in1=th[g][:], op=ALU.mult)
-
-        def f_A(g):
-            nc.vector.scalar_tensor_tensor(out=negA[g][:], in0=sq[g][:], scalar=1.0, in1=bank_b[g][:], op0=ALU.subtract, op1=ALU.mult)
-
-        def f_ln(g):
-            nc.scalar.activation(out=lnq[g][:], in_=esum[g][:], func=ACT.Ln, bias=1.0)
-
-        def f_L(g):
-            nc.vector.tensor_tensor(out=lse[g][:], in0=bank_a[g][:], in1=lnq[g][:], op=ALU.add)
-
-        def f_r(g):
-            nc.scalar.activation(out=p1[g][:], in_=lnq[g][:], func=ACT.Exp, scale=-1.0)
-
-        def f_m(g, eng):
-            eng.tensor_tensor(out=mm[g][:], in0=negA[g][:], in1=lse[g][:], op=ALU.mult)
-
-        def f_part(g):
-            nc.vector.tensor_tensor(out=part[g][:], in0=old_sb[:, g, :], in1=mm[g][:], op=ALU.subtract)
-
-        def f_n(g, lo, hi):
-            nc.vector.tensor_tensor(out=nn[g][:, lo:hi], in0=ct[g][:, lo:hi], in1=p1[g][:, lo:hi], op=ALU.mult)
-
-        def f_out(g, lo, hi):
-            nc.vector.tensor_tensor(out=res[g][:, lo:hi], in0=nn[g][:, lo:hi], in1=part[g][:, lo:hi], op=ALU.add)
-            nc.sync.dma_start(out=out[g, :, lo:hi], in_=res[g][:, lo:hi])
-
-        diff(bank_b, 0, (0, 1))
+        diff(bank_b, 0, range(G))
         for g in range(G):
-            f_tanh(g)
+            nc.scalar.activation(out=th[:, cols(g)], in_=bank_a[g][:], func=ACT.Tanh)
         diff(bank_a, M, (0, 1))
-        diff(bank_b, 0, (2, 3))
         diff(bank_a, M, (2, 3))
 
-        dst, src = views(wo_op, 0, wo_raw, 0, M)
-        nc.vector.tensor_copy(out=dst, in_=src)
-        f_sq_v(0)
-        quantize(wo_op)
-        dst, src = views(dy_op, 0, dy_raw, 0, N)
-        nc.vector.tensor_copy(out=dst, in_=src)
-        f_sq_v(1)
-        quantize(dy_op)
+        f_sq(0)
+        f_sq(1)
+        round_v(dy_op, 0, dy_raw, 0, N)
+        f_sq(2)
+        quantize(dy_op, 0, N)
+        f_sq(3)
 
-        f_e2(0)
-        f_e2(1)
-        f_c0(0)
-        f_c0(1)
-        f_e3(0)
-        f_e3(1)
-        f_z1(0)
-        f_z1(1)
-        f_e2(2)
-        f_e2(3)
-        f_c0(2)
-        f_c0(3)
-        f_e3(2)
-        f_e3(3)
-        f_z1(2)
-        f_z1(3)
-        f_sq_s(2)
-        f_sq_s(3)
-        f_D(0, nc.vector)
-        f_D(1, nc.vector)
-        f_ct(0)
-        f_ct(1)
-        f_A(0)
-        f_A(1)
-        f_ct(2)
-        f_D(2, nc.vector)
-        f_ct(3)
-        f_D(3, nc.vector)
-        f_A(2)
-        f_A(3)
+        esum0 = sb.tile([P, N], F32, name="esum0", tag="dy_bf", align_bytes=64)
+        esum123 = sb.tile([P, 3 * N], F32, name="esum123", align_bytes=64)
+        esum = [esum0[:]] + [esum123[:, cols(g)] for g in range(G - 1)]
+        for pair in ((0, 1), (2, 3)):
+            for g in pair:
+                nc.scalar.activation(out=e2[:, cols(g)], in_=bank_b[g][:], func=ACT.Exp)
+            for g in pair:
+                product(bank_b[g], g, wo_op, 0, dy_op, True, True)
+            for g in pair:
+                nc.scalar.activation(out=e3[:, cols(g)], in_=bank_a[g][:], func=ACT.Exp)
+            for g in pair:
+                product(bank_a[g], g, w1_op, 0, x_op, True, True)
+            for g in pair:
+                nc.gpsimd.tensor_tensor(out=esum[g], in0=e2[:, cols(g)], in1=e3[:, cols(g)], op=ALU.add)
+            for g in pair:
+                nc.vector.tensor_tensor(out=ct[:, cols(g)], in0=bank_b[g][:], in1=th[:, cols(g)], op=ALU.mult)
+            for g in pair:
+                nc.vector.scalar_tensor_tensor(
+                    out=negA[:, cols(g)], in0=sq[:, cols(g)], scalar=1.0, in1=bank_b[g][:], op0=ALU.subtract, op1=ALU.mult
+                )
         for g in range(G):
-            f_ln(g)
+            nc.scalar.activation(out=lnq[:, cols(g)], in_=esum[g], func=ACT.Ln, bias=1.0)
+        for g in (0, 2):
+            nc.scalar.activation(out=p1[:, cols(g, 2)], in_=lnq[:, cols(g, 2)], func=ACT.Exp, scale=-1.0)
         for g in range(G):
-            f_r(g)
-        f_L(0)
-        f_L(1)
-        f_m(0, nc.vector)
-        f_L(2)
-        f_m(1, nc.vector)
-        f_L(3)
-        f_part(0)
-        f_m(2, nc.vector)
-        f_part(1)
-        f_m(3, nc.vector)
-        f_n(0, 0, N)
-        f_part(2)
-        f_out(0, 0, N)
-        f_n(1, 0, N)
-        f_part(3)
-        f_out(1, 0, N)
-        f_n(2, 0, N)
-        f_n(3, 0, N)
-        f_out(2, 0, N)
-        f_out(3, 0, N // 2)
-        f_out(3, N // 2, N)
+            nc.vector.tensor_tensor(out=lse[:, cols(g)], in0=bank_a[g][:], in1=lnq[:, cols(g)], op=ALU.add)
+        f_m(nc.gpsimd, cols(0))
+        f_m(nc.gpsimd, slice(N, N + HALF))
+        f_m(nc.vector, slice(N + HALF, 2 * N))
+        f_m(nc.vector, cols(2, 2))
+        f_part(cols(0, 2))
+        f_n(cols(0, 2))
+        f_part(cols(2, 2))
+        f_out(cols(0, 2))
+        store(0, 0, N)
+        store(1, 0, N)
+        f_n(cols(2))
+        f_n(cols(3))
+        f_out(cols(2))
+        store(2, 0, N)
+        f_out(slice(3 * N, 3 * N + HALF))
+        store(3, 0, HALF)
+        f_out(slice(3 * N + HALF, 4 * N))
+        store(3, HALF, N)

@@ -17,7 +17,8 @@ P = 128
 PACK = 4
 ROWS = 32
 HALF = N // 2
-X_SPLIT = 176
+EARLY = (0, 1)
+LATE = (2, 3)
 
 
 def tile_rows_bsoftmaxthree_kernel(tc, x, w1, w2, w3, wo, dy, old, out):
@@ -78,8 +79,8 @@ def tile_rows_bsoftmaxthree_kernel(tc, x, w1, w2, w3, wo, dy, old, out):
             return slice(g * N, (g + n) * N)
 
         w1_raw = load("w1_raw", w1, 0, M)
-        xa_raw = load("xa_raw", x, 0, HALF)
-        xb_raw = load("xb_raw", x, HALF, N)
+        x_raw0 = load("x_raw0", x, 0, 256)
+        x_raw1 = load("x_raw1", x, 256, 512)
         w2_raw = load("w2_raw", w2, 0, M)
         w3_raw = load("w3_raw", w3, 0, M)
         wo_raw = load("wo_raw", wo, 0, M)
@@ -113,97 +114,147 @@ def tile_rows_bsoftmaxthree_kernel(tc, x, w1, w2, w3, wo, dy, old, out):
         dst, src = views(w1_op, M, w1_raw, 0, M)
         nc.vector.tensor_scalar(out=dst, in0=src, scalar1=-1.0, scalar2=None, op0=ALU.mult)
         quantize(w1_op, 0, 2 * M)
-        round_v(x_op, 0, xa_raw, 0, HALF)
-        quantize(x_op, 0, HALF)
-        round_s(x_op, HALF, xb_raw, X_SPLIT, HALF)
-        round_v(x_op, HALF, xb_raw, 0, X_SPLIT)
-        quantize(x_op, HALF, N)
-        for g in range(G):
+        round_v(x_op, 0, x_raw0, 0, 256)
+        quantize(x_op, 0, 256)
+        round_s(x_op, 256, x_raw1, 176, 256)
+        round_v(x_op, 256, x_raw1, 0, 176)
+        quantize(x_op, 256, 512)
+
+        d2_bank = [bank_b[0], bank_b[1], bank_a[2], bank_a[3]]
+        d3_bank = [bank_a[0], bank_a[1], bank_b[2], bank_b[3]]
+
+        def minus_z1(banks, groups):
+            for g in groups:
+                product(banks[g], g, w1_op, M, x_op, True, False)
+
+        def plus_z(banks, at, groups):
+            for g in groups:
+                product(banks[g], g, w23_op, at, x_op, False, True)
+
+        def tt(eng, dst, a, b, op):
+            eng.tensor_tensor(out=dst, in0=a, in1=b, op=op)
+
+        def f_tanh(g):
+            nc.scalar.activation(out=th[:, cols(g)], in_=bank_a[g][:], func=ACT.Tanh)
+
+        def f_e2(g):
+            nc.scalar.activation(out=e2[:, cols(g)], in_=d2_bank[g][:], func=ACT.Exp)
+
+        def f_e3(g):
+            nc.scalar.activation(out=e3[:, cols(g)], in_=d3_bank[g][:], func=ACT.Exp)
+
+        def f_z1(g):
             product(bank_a[g], g, w1_op, 0, x_op, True, True)
-        round_s(w23_op, 0, w2_raw, 0, M)
-        round_s(w23_op, M, w3_raw, 0, M)
-        round_v(wo_op, 0, wo_raw, 0, M)
-        quantize(w23_op, 0, 2 * M)
-        quantize(wo_op, 0, M)
 
-        def diff(banks, at, groups):
-            for g in groups:
-                product(banks[g], g, w23_op, at, x_op, True, False)
-            for g in groups:
-                product(banks[g], g, w1_op, M, x_op, False, True)
+        def f_c0(g):
+            product(bank_b[g], g, wo_op, 0, dy_op, True, True)
 
-        def f_sq(g):
-            nc.vector.tensor_tensor(out=sq[:, cols(g)], in0=th[:, cols(g)], in1=th[:, cols(g)], op=ALU.mult)
-
-        def f_m(eng, s):
-            eng.tensor_tensor(out=mm[:, s], in0=negA[:, s], in1=lse[:, s], op=ALU.mult)
-
-        def f_part(s):
-            nc.vector.tensor_tensor(out=part[:, s], in0=old_sb[:, s], in1=mm[:, s], op=ALU.subtract)
-
-        def f_n(s):
-            nc.vector.tensor_tensor(out=nn[:, s], in0=ct[:, s], in1=p1[:, s], op=ALU.mult)
-
-        def f_out(s):
-            nc.vector.tensor_tensor(out=res[:, s], in0=nn[:, s], in1=part[:, s], op=ALU.add)
+        def f_r(s):
+            nc.scalar.activation(out=p1[:, s], in_=lnq[:, s], func=ACT.Exp, scale=-1.0)
 
         def store(g, lo, hi):
             nc.sync.dma_start(out=out[g, :, lo:hi], in_=res[:, g * N + lo : g * N + hi])
 
-        diff(bank_b, 0, range(G))
-        for g in range(G):
-            nc.scalar.activation(out=th[:, cols(g)], in_=bank_a[g][:], func=ACT.Tanh)
-        diff(bank_a, M, (0, 1))
-        diff(bank_a, M, (2, 3))
-
-        f_sq(0)
-        f_sq(1)
+        for g in EARLY:
+            f_z1(g)
+        minus_z1(d2_bank, LATE)
+        minus_z1(d2_bank, EARLY)
+        round_s(w23_op, 0, w2_raw, 0, M)
+        quantize(w23_op, 0, M)
+        plus_z(d2_bank, 0, LATE)
+        plus_z(d2_bank, 0, EARLY)
+        minus_z1(d3_bank, LATE)
+        round_v(w23_op, M, w3_raw, 0, M)
+        round_v(wo_op, 0, wo_raw, 0, M)
+        quantize(w23_op, M, 2 * M)
+        quantize(wo_op, 0, M)
+        for g in EARLY:
+            f_tanh(g)
+        minus_z1(d3_bank, EARLY)
+        plus_z(d3_bank, M, LATE)
+        plus_z(d3_bank, M, EARLY)
+        tt(nc.vector, sq[:, cols(0)], th[:, cols(0)], th[:, cols(0)], ALU.mult)
+        tt(nc.vector, sq[:, cols(1)], th[:, cols(1)], th[:, cols(1)], ALU.mult)
         round_v(dy_op, 0, dy_raw, 0, N)
-        f_sq(2)
+        esum = wide("esum")
+        for g in LATE:
+            f_e2(g)
+        for g in LATE:
+            f_z1(g)
+        for g in LATE:
+            f_e3(g)
+        tt(nc.vector, esum[:, cols(2)], e2[:, cols(2)], e3[:, cols(2)], ALU.add)
         quantize(dy_op, 0, N)
-        f_sq(3)
-
+        tt(nc.vector, esum[:, cols(3)], e2[:, cols(3)], e3[:, cols(3)], ALU.add)
         esum0 = sb.tile([P, N], F32, name="esum0", tag="dy_bf", align_bytes=64)
-        esum123 = sb.tile([P, 3 * N], F32, name="esum123", align_bytes=64)
-        esum = [esum0[:]] + [esum123[:, cols(g)] for g in range(G - 1)]
-        for pair in ((0, 1), (2, 3)):
-            for g in pair:
-                nc.scalar.activation(out=e2[:, cols(g)], in_=bank_b[g][:], func=ACT.Exp)
-            for g in pair:
-                product(bank_b[g], g, wo_op, 0, dy_op, True, True)
-            for g in pair:
-                nc.scalar.activation(out=e3[:, cols(g)], in_=bank_a[g][:], func=ACT.Exp)
-            for g in pair:
-                product(bank_a[g], g, w1_op, 0, x_op, True, True)
-            for g in pair:
-                nc.gpsimd.tensor_tensor(out=esum[g], in0=e2[:, cols(g)], in1=e3[:, cols(g)], op=ALU.add)
-            for g in pair:
-                nc.vector.tensor_tensor(out=ct[:, cols(g)], in0=bank_b[g][:], in1=th[:, cols(g)], op=ALU.mult)
-            for g in pair:
-                nc.vector.scalar_tensor_tensor(
-                    out=negA[:, cols(g)], in0=sq[:, cols(g)], scalar=1.0, in1=bank_b[g][:], op0=ALU.subtract, op1=ALU.mult
-                )
+        sums = [esum0[:], esum[:, cols(1)], esum[:, cols(2)], esum[:, cols(3)]]
+        for g in EARLY:
+            f_e2(g)
+            f_e3(g)
         for g in range(G):
-            nc.scalar.activation(out=lnq[:, cols(g)], in_=esum[g], func=ACT.Ln, bias=1.0)
-        for g in (0, 2):
-            nc.scalar.activation(out=p1[:, cols(g, 2)], in_=lnq[:, cols(g, 2)], func=ACT.Exp, scale=-1.0)
+            f_c0(g)
+        for g in EARLY:
+            f_z1(g)
+        for g in EARLY:
+            tt(nc.gpsimd, sums[g], e2[:, cols(g)], e3[:, cols(g)], ALU.add)
+        for g in EARLY:
+            tt(nc.vector, ct[:, cols(g)], bank_b[g][:], th[:, cols(g)], ALU.mult)
+        for g in EARLY:
+            nc.vector.scalar_tensor_tensor(
+                out=negA[:, cols(g)], in0=sq[:, cols(g)], scalar=1.0, in1=bank_b[g][:], op0=ALU.subtract, op1=ALU.mult
+            )
         for g in range(G):
-            nc.vector.tensor_tensor(out=lse[:, cols(g)], in0=bank_a[g][:], in1=lnq[:, cols(g)], op=ALU.add)
-        f_m(nc.gpsimd, cols(0))
-        f_m(nc.gpsimd, slice(N, N + HALF))
-        f_m(nc.vector, slice(N + HALF, 2 * N))
-        f_m(nc.vector, cols(2, 2))
-        f_part(cols(0, 2))
-        f_n(cols(0, 2))
-        f_part(cols(2, 2))
-        f_out(cols(0, 2))
-        store(0, 0, N)
-        store(1, 0, N)
-        f_n(cols(2))
-        f_n(cols(3))
-        f_out(cols(2))
-        store(2, 0, N)
-        f_out(slice(3 * N, 3 * N + HALF))
-        store(3, 0, HALF)
-        f_out(slice(3 * N + HALF, 4 * N))
-        store(3, HALF, N)
+            nc.scalar.activation(out=lnq[:, cols(g)], in_=sums[g], func=ACT.Ln, bias=1.0)
+        for g in range(G):
+            tt(nc.vector, lse[:, cols(g)], bank_a[g][:], lnq[:, cols(g)], ALU.add)
+        for g in EARLY:
+            f_r(cols(g))
+        for g in LATE:
+            f_tanh(g)
+        f_r(cols(2))
+        for g in LATE:
+            nc.scalar.activation(out=sq[:, cols(g)], in_=th[:, cols(g)], func=ACT.Square)
+        f_r(cols(3))
+
+        for eng, s in ((nc.gpsimd, slice(0, 512)), (nc.vector, slice(512, 2 * N))):
+            tt(eng, mm[:, s], negA[:, s], lse[:, s], ALU.mult)
+        for g in EARLY:
+            tt(nc.vector, part[:, cols(g)], old_sb[:, cols(g)], mm[:, cols(g)], ALU.subtract)
+        for g in EARLY:
+            tt(nc.vector, nn[:, cols(g)], ct[:, cols(g)], p1[:, cols(g)], ALU.mult)
+        for g in EARLY:
+            tt(nc.vector, res[:, cols(g)], nn[:, cols(g)], part[:, cols(g)], ALU.add)
+            store(g, 0, N)
+
+        def f_b(g):
+            nc.vector.scalar_tensor_tensor(
+                out=mm[:, cols(g)], in0=sq[:, cols(g)], scalar=1.0, in1=lse[:, cols(g)], op0=ALU.subtract, op1=ALU.mult
+            )
+
+        def f_u(g):
+            tt(nc.vector, nn[:, cols(g)], th[:, cols(g)], p1[:, cols(g)], ALU.mult)
+
+        def f_v(g):
+            tt(nc.vector, part[:, cols(g)], nn[:, cols(g)], mm[:, cols(g)], ALU.subtract)
+
+        def f_w(g, lo, hi):
+            s = slice(g * N + lo, g * N + hi)
+            tt(nc.vector, ct[:, s], bank_b[g][:, lo:hi], part[:, s], ALU.mult)
+
+        def f_out(g, lo, hi):
+            s = slice(g * N + lo, g * N + hi)
+            tt(nc.vector, res[:, s], ct[:, s], old_sb[:, s], ALU.add)
+            store(g, lo, hi)
+
+        f_u(2)
+        f_b(2)
+        f_b(3)
+        f_v(2)
+        f_u(3)
+        f_w(2, 0, N)
+        f_v(3)
+        f_out(2, 0, N)
+        f_w(3, 0, HALF)
+        f_w(3, HALF, N)
+        f_out(3, 0, HALF)
+        f_out(3, HALF, N)

@@ -88,7 +88,7 @@ def tile_rows_bsoftmaxthree_kernel(tc, x, w1, w2, w3, wo, dy, old, out):
         old_sb = wide("old_sb")
         nc.sync.dma_start(out=old_sb[:].rearrange("m (g n) -> m g n", g=G), in_=old.rearrange("g m n -> m g n"))
 
-        w1_op = operand("w1", 2 * M)
+        w1_op = operand("w1", M)
         w23_op = operand("w23", 2 * M)
         wo_op = operand("wo", M)
         x_op = operand("x", N)
@@ -110,10 +110,9 @@ def tile_rows_bsoftmaxthree_kernel(tc, x, w1, w2, w3, wo, dy, old, out):
         nn = wide("nn")
         res = wide("res")
 
-        round_v(w1_op, 0, w1_raw, 0, M)
-        dst, src = views(w1_op, M, w1_raw, 0, M)
+        dst, src = views(w1_op, 0, w1_raw, 0, M)
         nc.vector.tensor_scalar(out=dst, in0=src, scalar1=-1.0, scalar2=None, op0=ALU.mult)
-        quantize(w1_op, 0, 2 * M)
+        quantize(w1_op, 0, M)
         round_v(x_op, 0, x_raw0, 0, 256)
         quantize(x_op, 0, 256)
         round_s(x_op, 256, x_raw1, 176, 256)
@@ -125,7 +124,7 @@ def tile_rows_bsoftmaxthree_kernel(tc, x, w1, w2, w3, wo, dy, old, out):
 
         def minus_z1(banks, groups):
             for g in groups:
-                product(banks[g], g, w1_op, M, x_op, True, False)
+                product(banks[g], g, w1_op, 0, x_op, True, False)
 
         def plus_z(banks, at, groups):
             for g in groups:
@@ -135,7 +134,7 @@ def tile_rows_bsoftmaxthree_kernel(tc, x, w1, w2, w3, wo, dy, old, out):
             eng.tensor_tensor(out=dst, in0=a, in1=b, op=op)
 
         def f_tanh(g):
-            nc.scalar.activation(out=th[:, cols(g)], in_=bank_a[g][:], func=ACT.Tanh)
+            nc.scalar.activation(out=th[:, cols(g)], in_=bank_a[g][:], func=ACT.Tanh, scale=-1.0)
 
         def f_e2(g):
             nc.scalar.activation(out=e2[:, cols(g)], in_=d2_bank[g][:], func=ACT.Exp)
@@ -163,39 +162,34 @@ def tile_rows_bsoftmaxthree_kernel(tc, x, w1, w2, w3, wo, dy, old, out):
         quantize(w23_op, 0, M)
         plus_z(d2_bank, 0, LATE)
         plus_z(d2_bank, 0, EARLY)
-        minus_z1(d3_bank, LATE)
         round_v(w23_op, M, w3_raw, 0, M)
         round_v(wo_op, 0, wo_raw, 0, M)
         quantize(w23_op, M, 2 * M)
         quantize(wo_op, 0, M)
         for g in EARLY:
             f_tanh(g)
-        minus_z1(d3_bank, EARLY)
-        plus_z(d3_bank, M, LATE)
-        plus_z(d3_bank, M, EARLY)
+        for pair in (EARLY, LATE):
+            minus_z1(d3_bank, pair)
+            plus_z(d3_bank, M, pair)
         tt(nc.vector, sq[:, cols(0)], th[:, cols(0)], th[:, cols(0)], ALU.mult)
         tt(nc.vector, sq[:, cols(1)], th[:, cols(1)], th[:, cols(1)], ALU.mult)
         round_v(dy_op, 0, dy_raw, 0, N)
-        esum = wide("esum")
-        for g in LATE:
-            f_e2(g)
-        for g in LATE:
-            f_z1(g)
-        for g in LATE:
-            f_e3(g)
-        tt(nc.vector, esum[:, cols(2)], e2[:, cols(2)], e3[:, cols(2)], ALU.add)
         quantize(dy_op, 0, N)
-        tt(nc.vector, esum[:, cols(3)], e2[:, cols(3)], e3[:, cols(3)], ALU.add)
-        esum0 = sb.tile([P, N], F32, name="esum0", tag="dy_bf", align_bytes=64)
-        sums = [esum0[:], esum[:, cols(1)], esum[:, cols(2)], esum[:, cols(3)]]
-        for g in EARLY:
+        for g in LATE + EARLY:
             f_e2(g)
-            f_e3(g)
         for g in range(G):
+            f_e3(g)
+        for g in EARLY:
             f_c0(g)
-        for g in EARLY:
+        for g in range(G):
             f_z1(g)
+        for g in LATE:
+            f_c0(g)
+        esum = wide("esum")
+        sums = [esum[:, cols(0)], esum[:, cols(1)], e2[:, cols(1)], esum[:, cols(3)]]
         for g in EARLY:
+            tt(nc.vector, sums[g], e2[:, cols(g)], e3[:, cols(g)], ALU.add)
+        for g in LATE:
             tt(nc.gpsimd, sums[g], e2[:, cols(g)], e3[:, cols(g)], ALU.add)
         for g in EARLY:
             tt(nc.vector, ct[:, cols(g)], bank_b[g][:], th[:, cols(g)], ALU.mult)
@@ -206,7 +200,7 @@ def tile_rows_bsoftmaxthree_kernel(tc, x, w1, w2, w3, wo, dy, old, out):
         for g in range(G):
             nc.scalar.activation(out=lnq[:, cols(g)], in_=sums[g], func=ACT.Ln, bias=1.0)
         for g in range(G):
-            tt(nc.vector, lse[:, cols(g)], bank_a[g][:], lnq[:, cols(g)], ALU.add)
+            tt(nc.vector, lse[:, cols(g)], lnq[:, cols(g)], bank_a[g][:], ALU.subtract)
         for g in EARLY:
             f_r(cols(g))
         for g in LATE:

@@ -78,9 +78,8 @@ def tile_rows_bsoftmaxthree_kernel(tc, x, w1, w2, w3, wo, dy, old, out):
         def cols(g, n=1):
             return slice(g * N, (g + n) * N)
 
+        x_raw = load("x_raw", x, 0, N)
         w1_raw = load("w1_raw", w1, 0, M)
-        x_raw0 = load("x_raw0", x, 0, 256)
-        x_raw1 = load("x_raw1", x, 256, 512)
         w2_raw = load("w2_raw", w2, 0, M)
         w3_raw = load("w3_raw", w3, 0, M)
         wo_raw = load("wo_raw", wo, 0, M)
@@ -110,14 +109,12 @@ def tile_rows_bsoftmaxthree_kernel(tc, x, w1, w2, w3, wo, dy, old, out):
         nn = wide("nn")
         res = wide("res")
 
+        round_s(x_op, 0, x_raw, 336, N)
+        round_v(x_op, 0, x_raw, 0, 336)
         dst, src = views(w1_op, 0, w1_raw, 0, M)
         nc.vector.tensor_scalar(out=dst, in0=src, scalar1=-1.0, scalar2=None, op0=ALU.mult)
+        quantize(x_op, 0, N)
         quantize(w1_op, 0, M)
-        round_v(x_op, 0, x_raw0, 0, 256)
-        quantize(x_op, 0, 256)
-        round_s(x_op, 256, x_raw1, 176, 256)
-        round_v(x_op, 256, x_raw1, 0, 176)
-        quantize(x_op, 256, 512)
 
         d2_bank = [bank_b[0], bank_b[1], bank_a[2], bank_a[3]]
         d3_bank = [bank_a[0], bank_a[1], bank_b[2], bank_b[3]]
@@ -157,10 +154,10 @@ def tile_rows_bsoftmaxthree_kernel(tc, x, w1, w2, w3, wo, dy, old, out):
         for g in EARLY:
             f_z1(g)
         minus_z1(d2_bank, LATE)
-        minus_z1(d2_bank, EARLY)
         round_s(w23_op, 0, w2_raw, 0, M)
         quantize(w23_op, 0, M)
         plus_z(d2_bank, 0, LATE)
+        minus_z1(d2_bank, EARLY)
         plus_z(d2_bank, 0, EARLY)
         round_v(w23_op, M, w3_raw, 0, M)
         round_v(wo_op, 0, wo_raw, 0, M)

from contextlib import ExitStack

import concourse.mybir as mybir

G, D, M, N = 4, 128, 128, 512
FLOPS = 4 * 2 * G * D * M * N

F32 = mybir.dt.float32
BF16 = mybir.dt.bfloat16
U32 = mybir.dt.uint32
U8 = mybir.dt.uint8
FP8X4 = mybir.dt.float8_e4m3fn_x4
ACT = mybir.ActivationFunctionType
ALU = mybir.AluOpType

P = 128
PACK = 4
ROWS = 32
HALF = N // 2
EARLY = (0, 1)
LATE = (2, 3)


def tile_rows_bsoftmaxthree_kernel(tc, x, w1, w2, w3, wo, dy, old, out):
    nc = tc.nc
    with ExitStack() as ctx:
        sb = ctx.enter_context(tc.tile_pool(name="sb", bufs=1))
        ps = ctx.enter_context(tc.psum_pool(name="ps", bufs=1))
        ctx.enter_context(tc.manual_schedule())

        def load(name, src, lo, hi):
            raw = sb.tile([P, PACK, hi - lo], F32, name=name, align_bytes=64)
            rows = src.rearrange("g d c -> (g d) c").rearrange("(p j) c -> p j c", j=PACK)
            nc.sync.dma_start(out=raw[:], in_=rows[:, :, lo:hi])
            return raw

        def operand(name, width):
            rounded = sb.tile([P, width, PACK], BF16, name=name + "_bf", align_bytes=64)
            codes = sb.tile([P, width], U32, name=name + "_codes", align_bytes=64)
            scales = sb.tile([P, width], U8, name=name + "_scales", align_bytes=64)
            return rounded, codes, scales

        def views(op, at, raw, lo, hi):
            dst = op[0][:, at + lo : at + hi, :].rearrange("p (c i) j -> p c j i", i=4)
            src = raw[:, :, lo:hi].rearrange("p j (c i) -> p c j i", i=4)
            return dst, src

        def round_v(op, at, raw, lo, hi):
            dst, src = views(op, at, raw, lo, hi)
            nc.vector.tensor_copy(out=dst, in_=src)

        def round_s(op, at, raw, lo, hi):
            dst, src = views(op, at, raw, lo, hi)
            nc.scalar.activation(out=dst, in_=src, func=ACT.Copy)

        def quantize(op, lo, hi):
            nc.vector.quantize_mx(
                out=op[1][:, lo:hi].bitcast(FP8X4),
                scales=op[2][:, lo:hi],
                in_=op[0][:, lo:hi, :].rearrange("p c j -> p (c j)"),
            )

        def product(bank, g, weights, at, moving, start, stop):
            rows = slice(ROWS * g, ROWS * (g + 1))
            nc.tensor.matmul_mx(
                out=bank[:],
                lhsT=weights[1][rows, at : at + M].bitcast(FP8X4),
                lhsT_scale=weights[2][rows, at : at + M],
                rhs=moving[1][rows, :].bitcast(FP8X4),
                rhs_scale=moving[2][rows, :],
                start=start,
                stop=stop,
            )

        def wide(name):
            return sb.tile([P, G * N], F32, name=name, align_bytes=64)

        def cols(g, n=1):
            return slice(g * N, (g + n) * N)

        x_raw = load("x_raw", x, 0, N)
        w1_raw = load("w1_raw", w1, 0, M)
        w2_raw = load("w2_raw", w2, 0, M)
        w3_raw = load("w3_raw", w3, 0, M)
        wo_raw = load("wo_raw", wo, 0, M)
        dy_raw = load("dy_raw", dy, 0, N)
        old_sb = wide("old_sb")
        nc.sync.dma_start(out=old_sb[:].rearrange("m (g n) -> m g n", g=G), in_=old.rearrange("g m n -> m g n"))

        w1_op = operand("w1", M)
        w23_op = operand("w23", 2 * M)
        wo_op = operand("wo", M)
        x_op = operand("x", N)
        dy_op = operand("dy", N)

        bank_a = [ps.tile([P, N], F32, name="bank_a" + str(g)) for g in range(G)]
        bank_b = [ps.tile([P, N], F32, name="bank_b" + str(g)) for g in range(G)]
        th = wide("th")
        sq = wide("sq")
        e2 = wide("e2")
        e3 = wide("e3")
        ct = wide("ct")
        negA = wide("negA")
        lnq = wide("lnq")
        lse = wide("lse")
        p1 = wide("p1")
        mm = wide("mm")
        part = wide("part")
        nn = wide("nn")
        res = wide("res")

        round_s(x_op, 0, x_raw, 336, N)
        round_v(x_op, 0, x_raw, 0, 336)
        dst, src = views(w1_op, 0, w1_raw, 0, M)
        nc.vector.tensor_scalar(out=dst, in0=src, scalar1=-1.0, scalar2=None, op0=ALU.mult)
        quantize(x_op, 0, N)
        quantize(w1_op, 0, M)

        d2_bank = [bank_b[0], bank_b[1], bank_a[2], bank_a[3]]
        d3_bank = [bank_a[0], bank_a[1], bank_b[2], bank_b[3]]

        def minus_z1(banks, groups):
            for g in groups:
                product(banks[g], g, w1_op, 0, x_op, True, False)

        def plus_z(banks, at, groups):
            for g in groups:
                product(banks[g], g, w23_op, at, x_op, False, True)

        def tt(eng, dst, a, b, op):
            eng.tensor_tensor(out=dst, in0=a, in1=b, op=op)

        def f_tanh(g):
            nc.scalar.activation(out=th[:, cols(g)], in_=bank_a[g][:], func=ACT.Tanh, scale=-1.0)

        def f_e2(g):
            nc.scalar.activation(out=e2[:, cols(g)], in_=d2_bank[g][:], func=ACT.Exp)

        def f_e3(g):
            nc.scalar.activation(out=e3[:, cols(g)], in_=d3_bank[g][:], func=ACT.Exp)

        def f_z1(g):
            product(bank_a[g], g, w1_op, 0, x_op, True, True)

        def f_c0(g):
            product(bank_b[g], g, wo_op, 0, dy_op, True, True)

        def f_r(s):
            nc.scalar.activation(out=p1[:, s], in_=lnq[:, s], func=ACT.Exp, scale=-1.0)

        def store(g, lo, hi):
            nc.sync.dma_start(out=out[g, :, lo:hi], in_=res[:, g * N + lo : g * N + hi])

        for g in EARLY:
            f_z1(g)
        minus_z1(d2_bank, LATE)
        round_s(w23_op, 0, w2_raw, 0, M)
        quantize(w23_op, 0, M)
        plus_z(d2_bank, 0, LATE)
        minus_z1(d2_bank, EARLY)
        plus_z(d2_bank, 0, EARLY)
        round_v(w23_op, M, w3_raw, 0, M)
        round_v(wo_op, 0, wo_raw, 0, M)
        quantize(w23_op, M, 2 * M)
        quantize(wo_op, 0, M)
        for g in EARLY:
            f_tanh(g)
        for pair in (EARLY, LATE):
            minus_z1(d3_bank, pair)
            plus_z(d3_bank, M, pair)
        tt(nc.vector, sq[:, cols(0)], th[:, cols(0)], th[:, cols(0)], ALU.mult)
        tt(nc.vector, sq[:, cols(1)], th[:, cols(1)], th[:, cols(1)], ALU.mult)
        round_v(dy_op, 0, dy_raw, 0, N)
        quantize(dy_op, 0, N)
        for g in LATE + EARLY:
            f_e2(g)
        for g in range(G):
            f_e3(g)
        for g in EARLY:
            f_c0(g)
        for g in range(G):
            f_z1(g)
        for g in LATE:
            f_c0(g)
        esum = wide("esum")
        sums = [esum[:, cols(0)], esum[:, cols(1)], e2[:, cols(1)], esum[:, cols(3)]]
        for g in EARLY:
            tt(nc.vector, sums[g], e2[:, cols(g)], e3[:, cols(g)], ALU.add)
        for g in LATE:
            tt(nc.gpsimd, sums[g], e2[:, cols(g)], e3[:, cols(g)], ALU.add)
        for g in EARLY:
            tt(nc.vector, ct[:, cols(g)], bank_b[g][:], th[:, cols(g)], ALU.mult)
        for g in EARLY:
            nc.vector.scalar_tensor_tensor(
                out=negA[:, cols(g)], in0=sq[:, cols(g)], scalar=1.0, in1=bank_b[g][:], op0=ALU.subtract, op1=ALU.mult
            )
        for g in range(G):
            nc.scalar.activation(out=lnq[:, cols(g)], in_=sums[g], func=ACT.Ln, bias=1.0)
        for g in range(G):
            tt(nc.vector, lse[:, cols(g)], lnq[:, cols(g)], bank_a[g][:], ALU.subtract)
        for g in EARLY:
            f_r(cols(g))
        for g in LATE:
            f_tanh(g)
        f_r(cols(2))
        for g in LATE:
            nc.scalar.activation(out=sq[:, cols(g)], in_=th[:, cols(g)], func=ACT.Square)
        f_r(cols(3))

        for eng, s in ((nc.gpsimd, slice(0, 512)), (nc.vector, slice(512, 2 * N))):
            tt(eng, mm[:, s], negA[:, s], lse[:, s], ALU.mult)
        for g in EARLY:
            tt(nc.vector, part[:, cols(g)], old_sb[:, cols(g)], mm[:, cols(g)], ALU.subtract)
        for g in EARLY:
            tt(nc.vector, nn[:, cols(g)], ct[:, cols(g)], p1[:, cols(g)], ALU.mult)
        for g in EARLY:
            tt(nc.vector, res[:, cols(g)], nn[:, cols(g)], part[:, cols(g)], ALU.add)
            store(g, 0, N)

        def f_b(g):
            nc.vector.scalar_tensor_tensor(
                out=mm[:, cols(g)], in0=sq[:, cols(g)], scalar=1.0, in1=lse[:, cols(g)], op0=ALU.subtract, op1=ALU.mult
            )

        def f_u(g):
            tt(nc.vector, nn[:, cols(g)], th[:, cols(g)], p1[:, cols(g)], ALU.mult)

        def f_v(g):
            tt(nc.vector, part[:, cols(g)], nn[:, cols(g)], mm[:, cols(g)], ALU.subtract)

        def f_w(g, lo, hi):
            s = slice(g * N + lo, g * N + hi)
            tt(nc.vector, ct[:, s], bank_b[g][:, lo:hi], part[:, s], ALU.mult)

        def f_out(g, lo, hi):
            s = slice(g * N + lo, g * N + hi)
            tt(nc.vector, res[:, s], ct[:, s], old_sb[:, s], ALU.add)
            store(g, lo, hi)

        f_u(2)
        f_b(2)
        f_b(3)
        f_v(2)
        f_u(3)
        f_w(2, 0, N)
        f_v(3)
        f_out(2, 0, N)
        f_w(3, 0, HALF)
        f_w(3, HALF, N)
        f_out(3, 0, HALF)
        f_out(3, HALF, N)
